import numpy as np
import ml_dtypes


def mxq(x, axis, fmt="e4m3"):
    dtype, down = {"e4m3": (ml_dtypes.float8_e4m3fn, 7), "e5m2": (ml_dtypes.float8_e5m2, 14)}[fmt]
    v = np.moveaxis(np.asarray(x, np.float32).astype(ml_dtypes.bfloat16).astype(np.float64), axis, -1)
    blocks = v.reshape(v.shape[:-1] + (-1, 32))
    amax = np.abs(blocks).max(-1, keepdims=True)
    byte = np.maximum(np.where(amax > 0, np.frexp(amax)[1] - 1 + 127, 0) - down, 1)
    scale = np.exp2(byte - 127.0)
    codes = (blocks / scale).astype(np.float32).astype(dtype).astype(np.float64)
    return np.moveaxis((codes * scale).reshape(v.shape), -1, axis)


WIDE = False


def mx_kscale(k):
    if not WIDE:
        return np.ones(k)
    levels = np.array([10, -10, 5, -5, 0])
    if k % 512:
        return np.exp2(np.random.permutation(np.resize(levels, k // 32))).repeat(32)
    a = np.empty((k // 512, 16))
    for p in range(k // 512):
        a[p, :8] = np.random.permutation(np.resize(levels, 8))
        for g in range(8):
            far = levels[np.abs(levels - a[p, g]) >= 10]
            a[p, g + 8] = far[np.random.randint(len(far))]
    return np.exp2(a.ravel()).repeat(32)


def f64(x):
    return np.asarray(x).astype(np.float64)


def striped(idx):
    return np.tile(idx.reshape(-1, 16).T, (8, 1)).astype(np.uint16)


def unstriped(offs):
    return offs[:16].T.reshape(-1).astype(np.int64)


def striped8(idx):
    return np.concatenate([x.reshape(-1, 16).T for x in idx]).astype(np.uint16)


def runs(offs, k):
    lists = np.stack([offs[16 * r : 16 * r + 16].T.reshape(-1) for r in range(8)]).astype(np.int64)
    return lists[np.arange(k) % 512 // 64]


def pack_weight(w):
    k, n = w.shape
    w = f64(np.asarray(w, np.float32).astype(ml_dtypes.bfloat16)).reshape(k // 32, 32, n)
    amax = np.abs(w).max(1)
    byte = np.clip(np.where(amax > 0, np.frexp(amax)[1] - 1 + 127 - 7, 1), 1, 254)
    scaled = (w * np.exp2(127.0 - byte)[:, None, :]).reshape(k, n).astype(np.float32)
    words = np.ascontiguousarray(scaled.reshape(k // 512, 128, 4, n).transpose(0, 1, 3, 2)).astype(ml_dtypes.float8_e4m3fn).view(np.uint8)
    return words, np.ascontiguousarray(byte.astype(np.uint8).reshape(k // 512, 16, n))


def unpack_weight(words, scales):
    g, p, n, _ = words.shape
    vals = np.ascontiguousarray(words).view(ml_dtypes.float8_e4m3fn).astype(np.float64) * np.repeat(np.exp2(scales.astype(np.float64) - 127.0), 8, axis=1)[..., None]
    return vals.transpose(0, 1, 3, 2).reshape(g * 512, n)


E2M1 = np.array([0.0, 0.5, 1.0, 1.5, 2.0, 3.0, 4.0, 6.0, -0.0, -0.5, -1.0, -1.5, -2.0, -3.0, -4.0, -6.0])


def pack_fp4(w):
    k, n = w.shape
    w = f64(np.asarray(w, np.float32).astype(ml_dtypes.bfloat16)).reshape(k // 32, 32, n)
    amax = np.abs(w).max(1)
    mant, ex = np.frexp(amax / 6.0)
    byte = np.clip(np.where(amax > 0, np.where(mant > 0.5, ex, ex - 1) + 127, 1), 1, 254)
    scaled = (w * np.exp2(127.0 - byte)[:, None, :]).reshape(k, n).astype(np.float32)
    c = np.ascontiguousarray(scaled.reshape(k // 512, 128, 4, n).transpose(0, 1, 3, 2)).astype(ml_dtypes.float4_e2m1fn).view(np.uint8) & 0xF
    words = (c[..., 0::2] | (c[..., 1::2] << 4)).reshape(k // 512, 128, 2 * n)
    return np.ascontiguousarray(words), np.ascontiguousarray(byte.astype(np.uint8).reshape(k // 512, 16, n))


def unpack_fp4(words, scales):
    g, _, n = scales.shape
    words = np.ascontiguousarray(words).reshape(g, 128, n, 2)
    nib = np.empty((g, 128, n, 4), np.uint8)
    nib[..., 0::2] = words & 0xF
    nib[..., 1::2] = words >> 4
    vals = E2M1[nib] * np.repeat(np.exp2(scales.astype(np.float64) - 127.0), 8, axis=1)[..., None]
    return vals.transpose(0, 1, 3, 2).reshape(g * 512, n)


def sigmoid(v):
    return 1.0 / (1.0 + np.exp(-np.maximum(v, -700.0)))

def planes(y):
    n, m = y.shape
    v = y.astype(np.float32).astype(ml_dtypes.bfloat16).astype(np.float64).reshape(n // 32, 32, m)
    top = np.abs(v).max(1)
    byte = np.clip(np.where(top > 0, np.frexp(top)[1] - 1 + 127 - 7, 1), 1, 254)
    codes = (v * np.exp2(127.0 - byte)[:, None, :]).reshape(n, m).astype(np.float32).astype(ml_dtypes.float8_e4m3fn).view(np.uint8)
    words = codes.reshape(n // 512, 128, 4, m).transpose(0, 1, 3, 2)
    return np.ascontiguousarray(words), np.ascontiguousarray(byte.astype(np.uint8).reshape(n // 512, 16, m))


K, T, S, V, H = 512, 2048, 512, 512, 512


def setup_inputs():
    n = np.random.standard_normal
    s = mx_kscale(K)[:, None]
    u = mx_kscale(S)
    packed_xT = pack_weight(n((K, T)) * s)
    packed_w1 = pack_fp4(n((K, H)) / np.sqrt(K) / s)
    packed_w2 = pack_fp4(n((K, H)) / np.sqrt(K) / s)
    return {
        "x_words": packed_xT[0],
        "x_scales": packed_xT[1],
        "w1_words": packed_w1[0],
        "w1_scales": packed_w1[1],
        "w2_words": packed_w2[0],
        "w2_scales": packed_w2[1],
        "ga": (np.random.uniform(0.5, 1.5, (H, 1)) * u[:, None]).astype(np.float32),
        "gb": (np.random.uniform(0.5, 1.5, (H, 1)) / u[:, None]).astype(np.float32),
        "offs": striped8(np.random.randint(0, T, (8, S))),
        "two": striped(np.random.permutation(T)[:V]),
        "n1": striped8(np.stack([np.random.permutation(S) for _ in range(8)])),
        "n2": striped8(np.stack([np.random.permutation(S) for _ in range(8)])),
        "n3": striped(np.random.permutation(V)),
        "n4": striped8(np.stack([np.random.permutation(V) for _ in range(8)])),
        "n5": striped8(np.stack([np.random.permutation(V) for _ in range(8)])),
    }


def reference(x_words, x_scales, w1_words, w1_scales, w2_words, w2_scales, ga, gb, offs, two, n1, n2, n3, n4, n5):
    xq = unpack_weight(x_words, x_scales)[np.arange(K)[:, None], runs(offs, K)]
    a = unpack_fp4(w1_words, w1_scales).T @ xq
    z = f64(ga) * (a * (sigmoid(a[np.arange(H)[:, None], runs(n1, H)] - (a[np.arange(H)[:, None], runs(n2, H)]))))
    x_two = unpack_weight(x_words, x_scales)[:, unstriped(two)]
    b = unpack_fp4(w2_words, w2_scales).T @ x_two
    z2 = f64(gb) * (b - b[:, unstriped(n3)])
    s = 0.0625 * ((mxq(z, 0, "e4m3").T @ mxq(z2, 0, "e4m3")))
    st = s + 0.5 * (s[np.arange(S)[:, None], runs(n4, S)])
    out_0 = st - (st[np.arange(S)[:, None], runs(n5, S)])
    return (out_0,) + planes(out_0)

@@ -1,0 +1,239 @@
+from contextlib import ExitStack
+
+import concourse.mybir as mybir
+from concourse.masks import make_identity
+
+FLOPS = 3 * 2 * 512 * 512 * 512
+
+F32 = mybir.dt.float32
+BF16 = mybir.dt.bfloat16
+I32 = mybir.dt.int32
+U32 = mybir.dt.uint32
+U16 = mybir.dt.uint16
+U8 = mybir.dt.uint8
+FP8X4 = mybir.dt.float8_e4m3fn_x4
+FP4X4 = mybir.dt.float4_e2m1fn_x4
+MULT = mybir.AluOpType.mult
+ADD = mybir.AluOpType.add
+SUB = mybir.AluOpType.subtract
+COPY = mybir.ActivationFunctionType.Copy
+SIGMOID = mybir.ActivationFunctionType.Sigmoid
+
+P = 128
+T = 2048
+N = 512
+PLANES = 4
+HALVES = 2
+HALF = N // HALVES
+LIST_COLS = HALF // 16
+
+
+def tile_picked_hkqcmpdifhop_none_po_kernel(
+    tc, x_words, x_scales, w1_words, w1_scales, w2_words, w2_scales, ga, gb,
+    offs, two, n1, n2, n3, n4, n5, out_0, out_1, out_2,
+):
+    nc = tc.nc
+
+    with ExitStack() as ctx:
+        keep = ctx.enter_context(tc.tile_pool(name="keep", bufs=1))
+        psum = ctx.enter_context(tc.psum_pool(name="psum", bufs=1))
+
+        def load_list(src, name):
+            tile = keep.tile([P, N // 16], U16, name=name)
+            nc.sync.dma_start(tile[:], src)
+            return tile
+
+        def half_of(lst, h):
+            return lst[:, h * LIST_COLS : (h + 1) * LIST_COLS]
+
+        def fetch(on_vector, out, window, offsets):
+            if on_vector:
+                nc.vector.tensor_copy(out, window.indirect(offsets))
+            else:
+                nc.scalar.activation(out, window.indirect(offsets), COPY)
+
+        offs_sb = load_list(offs, "offs_sb")
+        xs_by_run = keep.tile([P, T], U8, align_bytes=64)
+        nc.vector.memset(xs_by_run[:].bitcast(I32), 0)
+        nc.scalar.dma_start(xs_by_run[0:P:8, :].bitcast(I32), x_scales[0].bitcast(I32))
+        two_sb = load_list(two, "two_sb")
+
+        ws_raw = keep.tile([P, 2, N], U8, align_bytes=64)
+        nc.gpsimd.memset(ws_raw[:].bitcast(I32), 0)
+        for i, src in enumerate((w1_scales, w2_scales)):
+            nc.gpsimd.dma_start(ws_raw[0:P:8, i, :].bitcast(I32), src[0].bitcast(I32))
+
+        ww_raw = [keep.tile([P, 2 * N], U8, align_bytes=64, name=f"ww_raw{i}") for i in range(2)]
+        nc.sync.dma_start(ww_raw[0][:].bitcast(I32), w1_words[0].bitcast(I32))
+        xw = keep.tile([P, T], U32, align_bytes=64)
+        nc.sync.dma_start(xw[:].bitcast(I32), x_words[0].rearrange("p n t -> p (n t)").bitcast(I32))
+        nc.sync.dma_start(ww_raw[1][:].bitcast(I32), w2_words[0].bitcast(I32))
+
+        gain_rows = keep.tile([P, P], F32)
+        nc.gpsimd.memset(gain_rows[:], 0.0)
+        for i, src in enumerate((ga, gb)):
+            nc.gpsimd.dma_start(
+                gain_rows[PLANES * i : PLANES * (i + 1), :].rearrange("t (b u) -> t b u", u=8),
+                src.rearrange("(b t u) o -> t b (u o)", t=PLANES, u=8),
+            )
+        ws = keep.tile([P, 2 * N], U8, align_bytes=64)
+        nc.gpsimd.memset(ws[:].bitcast(I32), 0)
+        xs = keep.tile([P, 2 * N], U8, align_bytes=64)
+        nc.gpsimd.memset(xs[:].bitcast(I32), 0)
+        identity = keep.tile([P, P], F32)
+        make_identity(nc, identity[:])
+
+        a_sb = [keep.tile([P, 2 * N], F32, name=f"a_sb{t}") for t in range(PLANES)]
+        for t in range(PLANES):
+            nc.vector.memset(a_sb[t][:, N:], 0.0)
+
+        xs_picked = keep.tile([P, 2 * N], U8, align_bytes=64)
+        nc.vector.tensor_copy(xs_picked[:, :N], xs_by_run[:].indirect(offs_sb[:]))
+        nc.vector.tensor_copy(xs_picked[:, N:], xs_by_run[:].indirect(two_sb[:]))
+        ws_dealt = keep.tile([P, 2, N], U8, align_bytes=64)
+        nc.vector.tensor_copy(
+            ws_dealt[:].bitcast(I32).rearrange("p i (t b w) -> p i t b w", t=PLANES, w=2),
+            ws_raw[:].bitcast(I32).rearrange("p i (b t w) -> p i t b w", t=PLANES, w=2),
+        )
+        for q in range(4):
+            nc.sync.dma_start(
+                xs[32 * q : 32 * q + 4, :].bitcast(I32),
+                xs_picked[32 * q : 32 * q + 32 : 8, :].bitcast(I32),
+            )
+            nc.scalar.dma_start(
+                ws[32 * q : 32 * q + 4, :].bitcast(I32),
+                ws_dealt[32 * q : 32 * q + 32 : 8].rearrange("p i n -> p (i n)").bitcast(I32),
+            )
+
+        ww = [keep.tile([P, 2 * N], U8, align_bytes=64, name=f"ww{i}") for i in range(2)]
+
+        def deal_words(i):
+            nc.vector.tensor_copy(
+                ww[i][:].bitcast(I32).rearrange("p (t b w) -> p t b w", t=PLANES, w=4),
+                ww_raw[i][:].bitcast(I32).rearrange("p (b t w) -> p t b w", t=PLANES, w=4),
+            )
+
+        deal_words(0)
+        deal_words(1)
+        xw_offs = keep.tile([P, N], U32, align_bytes=64)
+        nc.vector.tensor_copy(xw_offs[:], xw[:].indirect(offs_sb[:]))
+        xw_two = keep.tile([P, N], U32, align_bytes=64)
+        nc.vector.tensor_copy(xw_two[:], xw[:].indirect(two_sb[:]))
+
+        n2_sb = load_list(n2, "n2_sb")
+        n1_sb = load_list(n1, "n1_sb")
+        n3_sb = load_list(n3, "n3_sb")
+        n4_sb = load_list(n4, "n4_sb")
+        n5_sb = load_list(n5, "n5_sb")
+
+        def project(i, t, words, name):
+            bank = psum.tile([P, N], F32, name=name, tag=name)
+            nc.tensor.matmul_mx(
+                out=bank[:],
+                lhsT=ww[i][:, 2 * P * t : 2 * P * (t + 1)].bitcast(FP4X4),
+                lhsT_scale=ws[:, i * N + P * t : i * N + P * (t + 1)],
+                rhs=words[:].bitcast(FP8X4),
+                rhs_scale=xs[:, i * N : (i + 1) * N],
+                start=True,
+                stop=True,
+            )
+            return bank
+
+        gain_bank = psum.tile([P, P], F32, name="gain_bank", tag="bank_b3")
+        nc.tensor.transpose(gain_bank[:], gain_rows[:], identity[:])
+        gains = keep.tile([P, 2 * PLANES], F32)
+        nc.scalar.copy(gains[:], gain_bank[:, : 2 * PLANES])
+
+        a_bank = [project(0, t, xw_offs, f"bank_a{t}") for t in range(PLANES)]
+        b_bank = [project(1, t, xw_two, f"bank_b{t}") for t in range(PLANES)]
+        b_sb = keep.tile([P, PLANES, N], F32)
+        for t in range(PLANES):
+            nc.vector.tensor_scalar(b_sb[:, t, :], b_bank[t][:], gains[:, PLANES + t : PLANES + t + 1], None, MULT)
+
+        z_planes = keep.tile([P, PLANES, N], BF16)
+        st_sb = [keep.tile([P, 2 * N], F32, name=f"st_sb{t}") for t in range(PLANES)]
+        half_s = [keep.tile([P, 2 * N], F32, name=f"half_s{t}") for t in range(PLANES)]
+        for t in range(PLANES):
+            nc.scalar.copy(a_sb[t][:, :N], a_bank[t][:])
+            at_n2 = st_sb[t][:, N:]
+            fetch(False, at_n2, a_sb[t][:], n2_sb[:])
+            diff = half_s[t][:, N:]
+            nc.vector.tensor_tensor(diff, a_sb[t][:].indirect(n1_sb[:]), at_n2, SUB)
+            sig = keep.tile([P, N], F32, name=f"sig{t}")
+            nc.scalar.activation(sig[:], diff, SIGMOID)
+            nc.vector.scalar_tensor_tensor(z_planes[:, t, :], a_bank[t][:], gains[:, t : t + 1], sig[:], MULT, MULT)
+        z_in = keep.tile([P, PLANES, P, PLANES], BF16, align_bytes=64)
+        nc.vector.tensor_copy(
+            z_in[:].rearrange("p c (a b) t -> p a c b t", b=2),
+            z_planes[:].rearrange("p t (a b c) -> p a c b t", b=2, c=PLANES),
+        )
+        z_words = keep.tile([P, N], U32, align_bytes=64)
+        z_scales = keep.tile([P, N], U8, align_bytes=64)
+        nc.vector.quantize_mx(
+            out=z_words[:].bitcast(FP8X4), scales=z_scales[:], in_=z_in[:].rearrange("p c m t -> p (c m t)")
+        )
+
+        z2_words = []
+        z2_scales = []
+        for h in range(HALVES):
+            cols = slice(h * HALF, (h + 1) * HALF)
+            at_n3 = keep.tile([P, PLANES, HALF], F32, name=f"at_n3_{h}")
+            for t in range(PLANES):
+                fetch(False, at_n3[:, t, :], b_sb[:, t, :], half_of(n3_sb, h))
+            z2_in = keep.tile([P, HALF, PLANES], BF16, align_bytes=64, name=f"z2_in{h}")
+            nc.vector.tensor_tensor(
+                z2_in[:].rearrange("p (c i) t -> p c t i", i=4),
+                b_sb[:, :, cols].rearrange("p t (c i) -> p c t i", i=4),
+                at_n3[:].rearrange("p t (c i) -> p c t i", i=4),
+                SUB,
+            )
+            words = keep.tile([P, HALF], U32, align_bytes=64, name=f"z2_words{h}")
+            scales = keep.tile([P, HALF], U8, align_bytes=64, name=f"z2_scales{h}")
+            nc.vector.quantize_mx(out=words[:].bitcast(FP8X4), scales=scales[:], in_=z2_in[:].rearrange("p v t -> p (v t)"))
+            z2_words.append(words)
+            z2_scales.append(scales)
+
+        s_bank = [psum.tile([P, N], F32, name=f"bank_s{t}", tag=f"bank_b{t}") for t in range(PLANES)]
+        for h in range(HALVES):
+            for t in range(PLANES):
+                nc.tensor.matmul_mx(
+                    out=s_bank[t][:, h * HALF : (h + 1) * HALF],
+                    lhsT=z_words[:, P * t : P * (t + 1)].bitcast(FP8X4),
+                    lhsT_scale=z_scales[:, P * t : P * (t + 1)],
+                    rhs=z2_words[h][:].bitcast(FP8X4),
+                    rhs_scale=z2_scales[h][:],
+                    start=True,
+                    stop=True,
+                )
+        for t in range(PLANES):
+            if t == 1:
+                nc.vector.tensor_scalar(half_s[t][:, :N], s_bank[t][:], 0.03125, None, MULT)
+            else:
+                nc.scalar.activation(half_s[t][:, :N], s_bank[t][:], COPY, scale=0.03125)
+            at_n4 = keep.tile([P, N], F32, name=f"at_n4_{t}")
+            fetch(t % 2 == 1, at_n4[:], half_s[t][:], n4_sb[:])
+            nc.vector.scalar_tensor_tensor(st_sb[t][:, :N], s_bank[t][:], 0.0625, at_n4[:], MULT, ADD)
+
+        y_words = keep.tile([P, N], U32, align_bytes=64)
+        y_scales = keep.tile([P, N], U8, align_bytes=64)
+        y_rows = out_0.rearrange("(p t) v -> p t v", t=PLANES)
+        y_codes = out_1[0].rearrange("p n t -> p (n t)").bitcast(I32)
+        for h in range(HALVES):
+            cols = slice(h * HALF, (h + 1) * HALF)
+            y = keep.tile([P, PLANES, HALF], F32, name=f"y{h}")
+            for t in range(PLANES):
+                at_n5 = keep.tile([P, HALF], F32, name=f"at_n5_{t}_{h}")
+                fetch(False, at_n5[:], st_sb[t][:], half_of(n5_sb, h))
+                nc.vector.tensor_tensor(y[:, t, :], st_sb[t][:, cols], at_n5[:], SUB)
+            nc.sync.dma_start(y_rows[:, :, cols], y[:])
+            y_in = keep.tile([P, HALF, PLANES], BF16, align_bytes=64, name=f"y_in{h}")
+            nc.vector.tensor_copy(
+                y_in[:].rearrange("p (c i) t -> p c t i", i=4), y[:].rearrange("p t (c i) -> p c t i", i=4)
+            )
+            nc.vector.quantize_mx(
+                out=y_words[:, cols].bitcast(FP8X4), scales=y_scales[:, cols], in_=y_in[:].rearrange("p v t -> p (v t)")
+            )
+            nc.sync.dma_start(y_codes[:, cols], y_words[:, cols].bitcast(I32))
+        for q in range(4):
+            queue = nc.scalar if q % 2 else nc.sync
+            queue.dma_start(out_2[0, 4 * q : 4 * q + 4, :].bitcast(I32), y_scales[32 * q : 32 * q + 4, :].bitcast(I32))

@@ -26,6 +26,7 @@ PLANES = 4
 HALVES = 2
 HALF = N // HALVES
 LIST_COLS = HALF // 16
+VECTOR_COLS = 384
 
 
 def tile_picked_hkqcmpdifhop_none_po_kernel(
@@ -52,22 +53,22 @@ def tile_picked_hkqcmpdifhop_none_po_kernel(
             else:
                 nc.scalar.activation(out, window.indirect(offsets), COPY)
 
+        def load_by_block(dst, rows):
+            words = rows.bitcast(I32)
+            nc.sync.dma_start(dst.bitcast(I32), words.unsqueeze(1).to_broadcast([16, 8, words.shape[1]]))
+
         offs_sb = load_list(offs, "offs_sb")
         xs_by_run = keep.tile([P, T], U8, align_bytes=64)
-        nc.vector.memset(xs_by_run[:].bitcast(I32), 0)
-        nc.scalar.dma_start(xs_by_run[0:P:8, :].bitcast(I32), x_scales[0].bitcast(I32))
+        load_by_block(xs_by_run[:], x_scales[0])
         two_sb = load_list(two, "two_sb")
-
         ws_raw = keep.tile([P, 2, N], U8, align_bytes=64)
-        nc.gpsimd.memset(ws_raw[:].bitcast(I32), 0)
         for i, src in enumerate((w1_scales, w2_scales)):
-            nc.gpsimd.dma_start(ws_raw[0:P:8, i, :].bitcast(I32), src[0].bitcast(I32))
-
-        ww_raw = [keep.tile([P, 2 * N], U8, align_bytes=64, name=f"ww_raw{i}") for i in range(2)]
-        nc.sync.dma_start(ww_raw[0][:].bitcast(I32), w1_words[0].bitcast(I32))
+            load_by_block(ws_raw[:, i, :], src[0])
         xw = keep.tile([P, T], U32, align_bytes=64)
         nc.sync.dma_start(xw[:].bitcast(I32), x_words[0].rearrange("p n t -> p (n t)").bitcast(I32))
-        nc.sync.dma_start(ww_raw[1][:].bitcast(I32), w2_words[0].bitcast(I32))
+        ww_raw = [keep.tile([P, 2 * N], U8, align_bytes=64, name=f"ww_raw{i}") for i in range(2)]
+        for tile, src in zip(ww_raw, (w1_words, w2_words)):
+            nc.sync.dma_start(tile[:].bitcast(I32), src[0].bitcast(I32))
 
         gain_rows = keep.tile([P, P], F32)
         nc.gpsimd.memset(gain_rows[:], 0.0)
@@ -77,15 +78,18 @@ def tile_picked_hkqcmpdifhop_none_po_kernel(
                 src.rearrange("(b t u) o -> t b (u o)", t=PLANES, u=8),
             )
         ws = keep.tile([P, 2 * N], U8, align_bytes=64)
-        nc.gpsimd.memset(ws[:].bitcast(I32), 0)
+        nc.vector.memset(ws[:].bitcast(I32), 0)
         xs = keep.tile([P, 2 * N], U8, align_bytes=64)
-        nc.gpsimd.memset(xs[:].bitcast(I32), 0)
+        nc.vector.memset(xs[:].bitcast(I32), 0)
         identity = keep.tile([P, P], F32)
         make_identity(nc, identity[:])
 
         a_sb = [keep.tile([P, 2 * N], F32, name=f"a_sb{t}") for t in range(PLANES)]
         for t in range(PLANES):
             nc.vector.memset(a_sb[t][:, N:], 0.0)
+
+        warm = keep.tile([P, 1], F32)
+        nc.scalar.activation(warm[:], a_sb[0][:, N : N + 1], SIGMOID)
 
         xs_picked = keep.tile([P, 2 * N], U8, align_bytes=64)
         nc.vector.tensor_copy(xs_picked[:, :N], xs_by_run[:].indirect(offs_sb[:]))
@@ -100,7 +104,7 @@ def tile_picked_hkqcmpdifhop_none_po_kernel(
                 xs[32 * q : 32 * q + 4, :].bitcast(I32),
                 xs_picked[32 * q : 32 * q + 32 : 8, :].bitcast(I32),
             )
-            nc.scalar.dma_start(
+            nc.sync.dma_start(
                 ws[32 * q : 32 * q + 4, :].bitcast(I32),
                 ws_dealt[32 * q : 32 * q + 32 : 8].rearrange("p i n -> p (i n)").bitcast(I32),
             )
@@ -142,13 +146,11 @@ def tile_picked_hkqcmpdifhop_none_po_kernel(
         gain_bank = psum.tile([P, P], F32, name="gain_bank", tag="bank_b3")
         nc.tensor.transpose(gain_bank[:], gain_rows[:], identity[:])
         gains = keep.tile([P, 2 * PLANES], F32)
-        nc.scalar.copy(gains[:], gain_bank[:, : 2 * PLANES])
+        nc.vector.tensor_copy(gains[:], gain_bank[:, : 2 * PLANES])
 
         a_bank = [project(0, t, xw_offs, f"bank_a{t}") for t in range(PLANES)]
         b_bank = [project(1, t, xw_two, f"bank_b{t}") for t in range(PLANES)]
         b_sb = keep.tile([P, PLANES, N], F32)
-        for t in range(PLANES):
-            nc.vector.tensor_scalar(b_sb[:, t, :], b_bank[t][:], gains[:, PLANES + t : PLANES + t + 1], None, MULT)
 
         z_planes = keep.tile([P, PLANES, N], BF16)
         st_sb = [keep.tile([P, 2 * N], F32, name=f"st_sb{t}") for t in range(PLANES)]
@@ -156,7 +158,7 @@ def tile_picked_hkqcmpdifhop_none_po_kernel(
         for t in range(PLANES):
             nc.scalar.copy(a_sb[t][:, :N], a_bank[t][:])
             at_n2 = st_sb[t][:, N:]
-            fetch(False, at_n2, a_sb[t][:], n2_sb[:])
+            fetch(t == 0, at_n2, a_sb[t][:], n2_sb[:])
             diff = half_s[t][:, N:]
             nc.vector.tensor_tensor(diff, a_sb[t][:].indirect(n1_sb[:]), at_n2, SUB)
             sig = keep.tile([P, N], F32, name=f"sig{t}")
@@ -173,13 +175,19 @@ def tile_picked_hkqcmpdifhop_none_po_kernel(
             out=z_words[:].bitcast(FP8X4), scales=z_scales[:], in_=z_in[:].rearrange("p c m t -> p (c m t)")
         )
 
+        for t in range(PLANES):
+            gain = gains[:, PLANES + t : PLANES + t + 1]
+            if t % 2:
+                nc.vector.tensor_scalar(b_sb[:, t, :], b_bank[t][:], gain, None, MULT)
+            else:
+                nc.scalar.activation(b_sb[:, t, :], b_bank[t][:], COPY, scale=gain)
         z2_words = []
         z2_scales = []
         for h in range(HALVES):
             cols = slice(h * HALF, (h + 1) * HALF)
             at_n3 = keep.tile([P, PLANES, HALF], F32, name=f"at_n3_{h}")
             for t in range(PLANES):
-                fetch(False, at_n3[:, t, :], b_sb[:, t, :], half_of(n3_sb, h))
+                fetch(h == 0 and t == 0, at_n3[:, t, :], b_sb[:, t, :], half_of(n3_sb, h))
             z2_in = keep.tile([P, HALF, PLANES], BF16, align_bytes=64, name=f"z2_in{h}")
             nc.vector.tensor_tensor(
                 z2_in[:].rearrange("p (c i) t -> p c t i", i=4),
@@ -193,11 +201,14 @@ def tile_picked_hkqcmpdifhop_none_po_kernel(
             z2_words.append(words)
             z2_scales.append(scales)
 
-        s_bank = [psum.tile([P, N], F32, name=f"bank_s{t}", tag=f"bank_b{t}") for t in range(PLANES)]
+        s_bank = [
+            [psum.tile([P, HALF], F32, name=f"bank_s{t}_{h}", tag=f"bank_{'ab'[h]}{t}") for t in range(PLANES)]
+            for h in range(HALVES)
+        ]
         for h in range(HALVES):
             for t in range(PLANES):
                 nc.tensor.matmul_mx(
-                    out=s_bank[t][:, h * HALF : (h + 1) * HALF],
+                    out=s_bank[h][t][:],
                     lhsT=z_words[:, P * t : P * (t + 1)].bitcast(FP8X4),
                     lhsT_scale=z_scales[:, P * t : P * (t + 1)],
                     rhs=z2_words[h][:].bitcast(FP8X4),
@@ -205,31 +216,37 @@ def tile_picked_hkqcmpdifhop_none_po_kernel(
                     start=True,
                     stop=True,
                 )
+        s_sb = [None] + [keep.tile([P, N], F32, name=f"s_sb{t}") for t in range(1, PLANES)]
+        first = slice(0, HALF)
+        second = slice(HALF, N)
         for t in range(PLANES):
-            if t == 1:
-                nc.vector.tensor_scalar(half_s[t][:, :N], s_bank[t][:], 0.03125, None, MULT)
-            else:
-                nc.scalar.activation(half_s[t][:, :N], s_bank[t][:], COPY, scale=0.03125)
-            at_n4 = keep.tile([P, N], F32, name=f"at_n4_{t}")
-            fetch(t % 2 == 1, at_n4[:], half_s[t][:], n4_sb[:])
-            nc.vector.scalar_tensor_tensor(st_sb[t][:, :N], s_bank[t][:], 0.0625, at_n4[:], MULT, ADD)
+            nc.scalar.activation(half_s[t][:, first], s_bank[0][t][:], COPY, scale=0.03125)
+            if t:
+                nc.scalar.activation(s_sb[t][:, first], s_bank[0][t][:], COPY, scale=0.0625)
+        nc.vector.tensor_scalar(half_s[0][:, second], s_bank[1][0][:], 0.03125, None, MULT)
+        at_n4 = keep.tile([P, N], F32)
+        nc.vector.tensor_copy(at_n4[:], half_s[0][:].indirect(n4_sb[:]))
+        for h, cols in enumerate((first, second)):
+            nc.vector.scalar_tensor_tensor(st_sb[0][:, cols], s_bank[h][0][:], 0.0625, at_n4[:, cols], MULT, ADD)
+        for t in range(1, PLANES):
+            nc.scalar.activation(half_s[t][:, second], s_bank[1][t][:], COPY, scale=0.03125)
+            nc.scalar.activation(s_sb[t][:, second], s_bank[1][t][:], COPY, scale=0.0625)
+            nc.vector.tensor_tensor(st_sb[t][:, :N], half_s[t][:].indirect(n4_sb[:]), s_sb[t][:], ADD)
+
+        y = keep.tile([P, PLANES, N], F32)
+        y_rows = out_0.rearrange("(p t) v -> p t v", t=PLANES)
+        for t in range(PLANES):
+            at_n5 = keep.tile([P, N], F32, name=f"at_n5_{t}")
+            nc.scalar.activation(at_n5[:], st_sb[t][:].indirect(n5_sb[:]), COPY)
+            nc.vector.tensor_tensor(y[:, t, :], st_sb[t][:, :N], at_n5[:], SUB)
+            nc.sync.dma_start(y_rows[:, t, :], y[:, t, :])
 
         y_words = keep.tile([P, N], U32, align_bytes=64)
         y_scales = keep.tile([P, N], U8, align_bytes=64)
-        y_rows = out_0.rearrange("(p t) v -> p t v", t=PLANES)
         y_codes = out_1[0].rearrange("p n t -> p (n t)").bitcast(I32)
-        for h in range(HALVES):
-            cols = slice(h * HALF, (h + 1) * HALF)
-            y = keep.tile([P, PLANES, HALF], F32, name=f"y{h}")
-            for t in range(PLANES):
-                at_n5 = keep.tile([P, HALF], F32, name=f"at_n5_{t}_{h}")
-                fetch(False, at_n5[:], st_sb[t][:], half_of(n5_sb, h))
-                nc.vector.tensor_tensor(y[:, t, :], st_sb[t][:, cols], at_n5[:], SUB)
-            nc.sync.dma_start(y_rows[:, :, cols], y[:])
-            y_in = keep.tile([P, HALF, PLANES], BF16, align_bytes=64, name=f"y_in{h}")
-            nc.vector.tensor_copy(
-                y_in[:].rearrange("p (c i) t -> p c t i", i=4), y[:].rearrange("p t (c i) -> p c t i", i=4)
-            )
+        for cols, weave in ((slice(0, VECTOR_COLS), nc.vector.tensor_copy), (slice(VECTOR_COLS, N), nc.scalar.copy)):
+            y_in = keep.tile([P, cols.stop - cols.start, PLANES], BF16, align_bytes=64, name=f"y_in{cols.start}")
+            weave(y_in[:].rearrange("p (c i) t -> p c t i", i=4), y[:, :, cols].rearrange("p t (c i) -> p c t i", i=4))
             nc.vector.quantize_mx(
                 out=y_words[:, cols].bitcast(FP8X4), scales=y_scales[:, cols], in_=y_in[:].rearrange("p v t -> p (v t)")
             )

from contextlib import ExitStack

import concourse.mybir as mybir
from concourse.masks import make_identity

FLOPS = 3 * 2 * 512 * 512 * 512

F32 = mybir.dt.float32
BF16 = mybir.dt.bfloat16
I32 = mybir.dt.int32
U32 = mybir.dt.uint32
U16 = mybir.dt.uint16
U8 = mybir.dt.uint8
FP8X4 = mybir.dt.float8_e4m3fn_x4
FP4X4 = mybir.dt.float4_e2m1fn_x4
MULT = mybir.AluOpType.mult
ADD = mybir.AluOpType.add
SUB = mybir.AluOpType.subtract
COPY = mybir.ActivationFunctionType.Copy
SIGMOID = mybir.ActivationFunctionType.Sigmoid

P = 128
T = 2048
N = 512
PLANES = 4
HALVES = 2
HALF = N // HALVES
LIST_COLS = HALF // 16
VECTOR_COLS = 384


def tile_picked_hkqcmpdifhop_none_po_kernel(
    tc, x_words, x_scales, w1_words, w1_scales, w2_words, w2_scales, ga, gb,
    offs, two, n1, n2, n3, n4, n5, out_0, out_1, out_2,
):
    nc = tc.nc

    with ExitStack() as ctx:
        keep = ctx.enter_context(tc.tile_pool(name="keep", bufs=1))
        psum = ctx.enter_context(tc.psum_pool(name="psum", bufs=1))

        def load_list(src, name):
            tile = keep.tile([P, N // 16], U16, name=name)
            nc.sync.dma_start(tile[:], src)
            return tile

        def half_of(lst, h):
            return lst[:, h * LIST_COLS : (h + 1) * LIST_COLS]

        def fetch(on_vector, out, window, offsets):
            if on_vector:
                nc.vector.tensor_copy(out, window.indirect(offsets))
            else:
                nc.scalar.activation(out, window.indirect(offsets), COPY)

        def load_by_block(dst, rows):
            words = rows.bitcast(I32)
            nc.sync.dma_start(dst.bitcast(I32), words.unsqueeze(1).to_broadcast([16, 8, words.shape[1]]))

        offs_sb = load_list(offs, "offs_sb")
        xs_by_run = keep.tile([P, T], U8, align_bytes=64)
        load_by_block(xs_by_run[:], x_scales[0])
        two_sb = load_list(two, "two_sb")
        ws_raw = keep.tile([P, 2, N], U8, align_bytes=64)
        for i, src in enumerate((w1_scales, w2_scales)):
            load_by_block(ws_raw[:, i, :], src[0])
        xw = keep.tile([P, T], U32, align_bytes=64)
        nc.sync.dma_start(xw[:].bitcast(I32), x_words[0].rearrange("p n t -> p (n t)").bitcast(I32))
        ww_raw = [keep.tile([P, 2 * N], U8, align_bytes=64, name=f"ww_raw{i}") for i in range(2)]
        for tile, src in zip(ww_raw, (w1_words, w2_words)):
            nc.sync.dma_start(tile[:].bitcast(I32), src[0].bitcast(I32))

        gain_rows = keep.tile([P, P], F32)
        nc.gpsimd.memset(gain_rows[:], 0.0)
        for i, src in enumerate((ga, gb)):
            nc.gpsimd.dma_start(
                gain_rows[PLANES * i : PLANES * (i + 1), :].rearrange("t (b u) -> t b u", u=8),
                src.rearrange("(b t u) o -> t b (u o)", t=PLANES, u=8),
            )
        ws = keep.tile([P, 2 * N], U8, align_bytes=64)
        nc.vector.memset(ws[:].bitcast(I32), 0)
        xs = keep.tile([P, 2 * N], U8, align_bytes=64)
        nc.vector.memset(xs[:].bitcast(I32), 0)
        identity = keep.tile([P, P], F32)
        make_identity(nc, identity[:])

        a_sb = [keep.tile([P, 2 * N], F32, name=f"a_sb{t}") for t in range(PLANES)]
        for t in range(PLANES):
            nc.vector.memset(a_sb[t][:, N:], 0.0)

        warm = keep.tile([P, 1], F32)
        nc.scalar.activation(warm[:], a_sb[0][:, N : N + 1], SIGMOID)

        xs_picked = keep.tile([P, 2 * N], U8, align_bytes=64)
        nc.vector.tensor_copy(xs_picked[:, :N], xs_by_run[:].indirect(offs_sb[:]))
        nc.vector.tensor_copy(xs_picked[:, N:], xs_by_run[:].indirect(two_sb[:]))
        ws_dealt = keep.tile([P, 2, N], U8, align_bytes=64)
        nc.vector.tensor_copy(
            ws_dealt[:].bitcast(I32).rearrange("p i (t b w) -> p i t b w", t=PLANES, w=2),
            ws_raw[:].bitcast(I32).rearrange("p i (b t w) -> p i t b w", t=PLANES, w=2),
        )
        for q in range(4):
            nc.sync.dma_start(
                xs[32 * q : 32 * q + 4, :].bitcast(I32),
                xs_picked[32 * q : 32 * q + 32 : 8, :].bitcast(I32),
            )
            nc.sync.dma_start(
                ws[32 * q : 32 * q + 4, :].bitcast(I32),
                ws_dealt[32 * q : 32 * q + 32 : 8].rearrange("p i n -> p (i n)").bitcast(I32),
            )

        ww = [keep.tile([P, 2 * N], U8, align_bytes=64, name=f"ww{i}") for i in range(2)]

        def deal_words(i):
            nc.vector.tensor_copy(
                ww[i][:].bitcast(I32).rearrange("p (t b w) -> p t b w", t=PLANES, w=4),
                ww_raw[i][:].bitcast(I32).rearrange("p (b t w) -> p t b w", t=PLANES, w=4),
            )

        deal_words(0)
        deal_words(1)
        xw_offs = keep.tile([P, N], U32, align_bytes=64)
        nc.vector.tensor_copy(xw_offs[:], xw[:].indirect(offs_sb[:]))
        xw_two = keep.tile([P, N], U32, align_bytes=64)
        nc.vector.tensor_copy(xw_two[:], xw[:].indirect(two_sb[:]))

        n2_sb = load_list(n2, "n2_sb")
        n1_sb = load_list(n1, "n1_sb")
        n3_sb = load_list(n3, "n3_sb")
        n4_sb = load_list(n4, "n4_sb")
        n5_sb = load_list(n5, "n5_sb")

        def project(i, t, words, name):
            bank = psum.tile([P, N], F32, name=name, tag=name)
            nc.tensor.matmul_mx(
                out=bank[:],
                lhsT=ww[i][:, 2 * P * t : 2 * P * (t + 1)].bitcast(FP4X4),
                lhsT_scale=ws[:, i * N + P * t : i * N + P * (t + 1)],
                rhs=words[:].bitcast(FP8X4),
                rhs_scale=xs[:, i * N : (i + 1) * N],
                start=True,
                stop=True,
            )
            return bank

        gain_bank = psum.tile([P, P], F32, name="gain_bank", tag="bank_b3")
        nc.tensor.transpose(gain_bank[:], gain_rows[:], identity[:])
        gains = keep.tile([P, 2 * PLANES], F32)
        nc.vector.tensor_copy(gains[:], gain_bank[:, : 2 * PLANES])

        a_bank = [project(0, t, xw_offs, f"bank_a{t}") for t in range(PLANES)]
        b_bank = [project(1, t, xw_two, f"bank_b{t}") for t in range(PLANES)]
        b_sb = keep.tile([P, PLANES, N], F32)

        z_planes = keep.tile([P, PLANES, N], BF16)
        st_sb = [keep.tile([P, 2 * N], F32, name=f"st_sb{t}") for t in range(PLANES)]
        half_s = [keep.tile([P, 2 * N], F32, name=f"half_s{t}") for t in range(PLANES)]
        for t in range(PLANES):
            nc.scalar.copy(a_sb[t][:, :N], a_bank[t][:])
            at_n2 = st_sb[t][:, N:]
            fetch(t == 0, at_n2, a_sb[t][:], n2_sb[:])
            diff = half_s[t][:, N:]
            nc.vector.tensor_tensor(diff, a_sb[t][:].indirect(n1_sb[:]), at_n2, SUB)
            sig = keep.tile([P, N], F32, name=f"sig{t}")
            nc.scalar.activation(sig[:], diff, SIGMOID)
            nc.vector.scalar_tensor_tensor(z_planes[:, t, :], a_bank[t][:], gains[:, t : t + 1], sig[:], MULT, MULT)
        z_in = keep.tile([P, PLANES, P, PLANES], BF16, align_bytes=64)
        nc.vector.tensor_copy(
            z_in[:].rearrange("p c (a b) t -> p a c b t", b=2),
            z_planes[:].rearrange("p t (a b c) -> p a c b t", b=2, c=PLANES),
        )
        z_words = keep.tile([P, N], U32, align_bytes=64)
        z_scales = keep.tile([P, N], U8, align_bytes=64)
        nc.vector.quantize_mx(
            out=z_words[:].bitcast(FP8X4), scales=z_scales[:], in_=z_in[:].rearrange("p c m t -> p (c m t)")
        )

        for t in range(PLANES):
            gain = gains[:, PLANES + t : PLANES + t + 1]
            if t % 2:
                nc.vector.tensor_scalar(b_sb[:, t, :], b_bank[t][:], gain, None, MULT)
            else:
                nc.scalar.activation(b_sb[:, t, :], b_bank[t][:], COPY, scale=gain)
        z2_words = []
        z2_scales = []
        for h in range(HALVES):
            cols = slice(h * HALF, (h + 1) * HALF)
            at_n3 = keep.tile([P, PLANES, HALF], F32, name=f"at_n3_{h}")
            for t in range(PLANES):
                fetch(h == 0 and t == 0, at_n3[:, t, :], b_sb[:, t, :], half_of(n3_sb, h))
            z2_in = keep.tile([P, HALF, PLANES], BF16, align_bytes=64, name=f"z2_in{h}")
            nc.vector.tensor_tensor(
                z2_in[:].rearrange("p (c i) t -> p c t i", i=4),
                b_sb[:, :, cols].rearrange("p t (c i) -> p c t i", i=4),
                at_n3[:].rearrange("p t (c i) -> p c t i", i=4),
                SUB,
            )
            words = keep.tile([P, HALF], U32, align_bytes=64, name=f"z2_words{h}")
            scales = keep.tile([P, HALF], U8, align_bytes=64, name=f"z2_scales{h}")
            nc.vector.quantize_mx(out=words[:].bitcast(FP8X4), scales=scales[:], in_=z2_in[:].rearrange("p v t -> p (v t)"))
            z2_words.append(words)
            z2_scales.append(scales)

        s_bank = [
            [psum.tile([P, HALF], F32, name=f"bank_s{t}_{h}", tag=f"bank_{'ab'[h]}{t}") for t in range(PLANES)]
            for h in range(HALVES)
        ]
        for h in range(HALVES):
            for t in range(PLANES):
                nc.tensor.matmul_mx(
                    out=s_bank[h][t][:],
                    lhsT=z_words[:, P * t : P * (t + 1)].bitcast(FP8X4),
                    lhsT_scale=z_scales[:, P * t : P * (t + 1)],
                    rhs=z2_words[h][:].bitcast(FP8X4),
                    rhs_scale=z2_scales[h][:],
                    start=True,
                    stop=True,
                )
        s_sb = [None] + [keep.tile([P, N], F32, name=f"s_sb{t}") for t in range(1, PLANES)]
        first = slice(0, HALF)
        second = slice(HALF, N)
        for t in range(PLANES):
            nc.scalar.activation(half_s[t][:, first], s_bank[0][t][:], COPY, scale=0.03125)
            if t:
                nc.scalar.activation(s_sb[t][:, first], s_bank[0][t][:], COPY, scale=0.0625)
        nc.vector.tensor_scalar(half_s[0][:, second], s_bank[1][0][:], 0.03125, None, MULT)
        at_n4 = keep.tile([P, N], F32)
        nc.vector.tensor_copy(at_n4[:], half_s[0][:].indirect(n4_sb[:]))
        for h, cols in enumerate((first, second)):
            nc.vector.scalar_tensor_tensor(st_sb[0][:, cols], s_bank[h][0][:], 0.0625, at_n4[:, cols], MULT, ADD)
        for t in range(1, PLANES):
            nc.scalar.activation(half_s[t][:, second], s_bank[1][t][:], COPY, scale=0.03125)
            nc.scalar.activation(s_sb[t][:, second], s_bank[1][t][:], COPY, scale=0.0625)
            nc.vector.tensor_tensor(st_sb[t][:, :N], half_s[t][:].indirect(n4_sb[:]), s_sb[t][:], ADD)

        y = keep.tile([P, PLANES, N], F32)
        y_rows = out_0.rearrange("(p t) v -> p t v", t=PLANES)
        for t in range(PLANES):
            at_n5 = keep.tile([P, N], F32, name=f"at_n5_{t}")
            nc.scalar.activation(at_n5[:], st_sb[t][:].indirect(n5_sb[:]), COPY)
            nc.vector.tensor_tensor(y[:, t, :], st_sb[t][:, :N], at_n5[:], SUB)
            nc.sync.dma_start(y_rows[:, t, :], y[:, t, :])

        y_words = keep.tile([P, N], U32, align_bytes=64)
        y_scales = keep.tile([P, N], U8, align_bytes=64)
        y_codes = out_1[0].rearrange("p n t -> p (n t)").bitcast(I32)
        for cols, weave in ((slice(0, VECTOR_COLS), nc.vector.tensor_copy), (slice(VECTOR_COLS, N), nc.scalar.copy)):
            y_in = keep.tile([P, cols.stop - cols.start, PLANES], BF16, align_bytes=64, name=f"y_in{cols.start}")
            weave(y_in[:].rearrange("p (c i) t -> p c t i", i=4), y[:, :, cols].rearrange("p t (c i) -> p c t i", i=4))
            nc.vector.quantize_mx(
                out=y_words[:, cols].bitcast(FP8X4), scales=y_scales[:, cols], in_=y_in[:].rearrange("p v t -> p (v t)")
            )
            nc.sync.dma_start(y_codes[:, cols], y_words[:, cols].bitcast(I32))
        for q in range(4):
            queue = nc.scalar if q % 2 else nc.sync
            queue.dma_start(out_2[0, 4 * q : 4 * q + 4, :].bitcast(I32), y_scales[32 * q : 32 * q + 4, :].bitcast(I32))
